import numpy as np
import ml_dtypes


def mxq(x, axis, fmt="e4m3"):
    dtype, down = {"e4m3": (ml_dtypes.float8_e4m3fn, 7), "e5m2": (ml_dtypes.float8_e5m2, 14)}[fmt]
    v = np.moveaxis(np.asarray(x, np.float32).astype(ml_dtypes.bfloat16).astype(np.float64), axis, -1)
    blocks = v.reshape(v.shape[:-1] + (-1, 32))
    amax = np.abs(blocks).max(-1, keepdims=True)
    byte = np.maximum(np.where(amax > 0, np.frexp(amax)[1] - 1 + 127, 0) - down, 1)
    scale = np.exp2(byte - 127.0)
    codes = (blocks / scale).astype(np.float32).astype(dtype).astype(np.float64)
    return np.moveaxis((codes * scale).reshape(v.shape), -1, axis)


WIDE = False


def mx_kscale(k):
    if not WIDE:
        return np.ones(k)
    levels = np.array([10, -10, 5, -5, 0])
    if k % 512:
        return np.exp2(np.random.permutation(np.resize(levels, k // 32))).repeat(32)
    a = np.empty((k // 512, 16))
    for p in range(k // 512):
        a[p, :8] = np.random.permutation(np.resize(levels, 8))
        for g in range(8):
            far = levels[np.abs(levels - a[p, g]) >= 10]
            a[p, g + 8] = far[np.random.randint(len(far))]
    return np.exp2(a.ravel()).repeat(32)


def f64(x):
    return np.asarray(x).astype(np.float64)


def striped(idx):
    return np.tile(idx.reshape(-1, 16).T, (8, 1)).astype(np.uint16)


def unstriped(offs):
    return offs[:16].T.reshape(-1).astype(np.int64)


E2M1 = np.array([0.0, 0.5, 1.0, 1.5, 2.0, 3.0, 4.0, 6.0, -0.0, -0.5, -1.0, -1.5, -2.0, -3.0, -4.0, -6.0])


def pack_weight(w, fmt):
    k, n = w.shape
    w = f64(np.asarray(w, np.float32).astype(ml_dtypes.bfloat16)).reshape(k // 32, 32, n)
    amax = np.abs(w).max(1)
    if fmt == "e4m3":
        byte = np.frexp(amax)[1] - 1 + 127 - 7
    else:
        mant, ex = np.frexp(amax / 6.0)
        byte = np.where(mant > 0.5, ex, ex - 1) + 127
    byte = np.clip(np.where(amax > 0, byte, 1), 1, 254)
    scaled = (w * np.exp2(127.0 - byte)[:, None, :]).reshape(k, n).astype(np.float32)
    by_word = np.ascontiguousarray(scaled.reshape(k // 512, 128, 4, n).transpose(0, 1, 3, 2))
    if fmt == "e4m3":
        words = by_word.astype(ml_dtypes.float8_e4m3fn).view(np.uint8)
    else:
        c = by_word.astype(ml_dtypes.float4_e2m1fn).view(np.uint8) & 0xF
        words = (c[..., 0::2] | (c[..., 1::2] << 4)).reshape(k // 512, 128, 2 * n)
    return np.ascontiguousarray(words), np.ascontiguousarray(byte.astype(np.uint8).reshape(k // 512, 16, n))


def unpack_weight(words, scales, fmt):
    g, _, n = scales.shape
    words = np.ascontiguousarray(words).reshape(g, 128, n, -1)
    if fmt == "e4m3":
        vals = words.view(ml_dtypes.float8_e4m3fn).astype(np.float64)
    else:
        nib = np.empty((g, 128, n, 4), np.uint8)
        nib[..., 0::2] = words & 0xF
        nib[..., 1::2] = words >> 4
        vals = E2M1[nib]
    vals = vals * np.repeat(np.exp2(scales.astype(np.float64) - 127.0), 8, axis=1)[..., None]
    return vals.transpose(0, 1, 3, 2).reshape(g * 512, n)


def gelu(v):
    return 0.5 * v * (1.0 + np.tanh(np.sqrt(2.0 / np.pi) * (v + 0.044715 * v**3)))


K, T, S, H, N = 1024, 2048, 512, 1536, 384


def setup_inputs():
    n = np.random.standard_normal
    s = mx_kscale(K)[:, None]
    u = mx_kscale(H)[:, None]
    tab_words, tab_scales = pack_weight(n((K, T)) * s, "e2m1")
    w2_words, w2_scales = pack_weight(n((K, H)) / np.sqrt(K) / s, "e4m3")
    w3_words, w3_scales = pack_weight(n((H, N)) / np.sqrt(H) / u, "e2m1")
    return {
        "tab_words": tab_words, "tab_scales": tab_scales,
        "offs": striped(np.random.permutation(T)[:S]),
        "offs2": striped(np.random.permutation(T)[:S]),
        "w1": (n((K, H)) / np.sqrt(K) / s).astype(np.float32),
        "w2_words": w2_words, "w2_scales": w2_scales,
        "ground": np.random.uniform(0.3, 1.0, H).astype(np.float32),
        "gain": (0.5 * np.random.uniform(1.0, 3.0, H) * u[:, 0]).astype(np.float32),
        "w3_words": w3_words, "w3_scales": w3_scales,
    }


def reference(tab_words, tab_scales, offs, offs2, w1, w2_words, w2_scales,
              ground, gain, w3_words, w3_scales):
    TW = unpack_weight(tab_words, tab_scales, "e2m1")
    v = TW[:, unstriped(offs)]
    v2 = TW[:, unstriped(offs2)]
    w2 = unpack_weight(w2_words, w2_scales, "e4m3")
    w3 = unpack_weight(w3_words, w3_scales, "e2m1")
    a = mxq(f64(w1), 0, "e4m3").T @ v
    b = w2.T @ v2
    e = np.square(a) + np.square(b) + f64(ground)[:, None]
    h = f64(gain)[:, None] * np.log(e)
    return w3.T @ mxq(h, 0, "e4m3")

@@ -1,0 +1,214 @@
+from contextlib import ExitStack
+
+import concourse.mybir as mybir
+from concourse.masks import make_identity
+
+K, T, S, H, N = 1024, 2048, 512, 1536, 384
+FLOPS = 2 * (2 * K * H * S + H * N * S)
+
+F32 = mybir.dt.float32
+BF16 = mybir.dt.bfloat16
+I32 = mybir.dt.int32
+U32 = mybir.dt.uint32
+U16 = mybir.dt.uint16
+U8 = mybir.dt.uint8
+FP8X4 = mybir.dt.float8_e4m3fn_x4
+FP4X4 = mybir.dt.float4_e2m1fn_x4
+ACT = mybir.ActivationFunctionType
+MULT = mybir.AluOpType.mult
+
+P = 128
+PACK = 4
+PASS = P * PACK
+KP = K // PASS
+G = H // PASS
+JT = S // P
+NT = N // P
+RUN = 4
+SHIFT_ROWS = 112
+
+
+def tile_list_scour_priority_kernel(
+    tc, tab_words, tab_scales, offs, offs2, w1, w2_words, w2_scales, ground, gain, w3_words, w3_scales, out
+):
+    nc = tc.nc
+    with ExitStack() as ctx:
+        keep = ctx.enter_context(tc.tile_pool(name="keep", bufs=1))
+        ring = ctx.enter_context(tc.tile_pool(name="ring", bufs=3))
+        psum = ctx.enter_context(tc.psum_pool(name="psum", bufs=4))
+
+        def held(name, shape, dtype):
+            return keep.tile(shape, dtype, name=name, align_bytes=64)
+
+        list_a = keep.tile([P, S // 16], U16, name="list_a")
+        list_b = keep.tile([P, S // 16], U16, name="list_b")
+        tab_w = [held("tab_w%d" % a, [P, T], U16) for a in range(KP)]
+        tab_s = held("tab_s", [P, T], U8)
+        w2_w = [held("w2_w%d" % g, [P, KP, PASS], U32) for g in range(G)]
+        w2_s = held("w2_s", [P, KP, H], U8)
+        w3_w = held("w3_w", [P, G, 2 * N], U8)
+        w3_s = held("w3_s", [P, G, N], U8)
+        ground_t = held("ground_t", [P, G, PACK], F32)
+        gain_t = held("gain_t", [P, G, PACK], F32)
+        ident = held("ident", [P, P], F32)
+        one = held("one", [P, 1], F32)
+        zero = held("zero", [P, 1], F32)
+        picked_w = {(x, a): held("picked_w%s%d" % (x, a), [P, S], U16) for x in "ab" for a in range(KP)}
+        picked_s = {(x, a): held("picked_s%s%d" % (x, a), [P, S], U8) for x in "ab" for a in range(KP)}
+        w1_raw = {(g, a): held("w1_raw%d%d" % (g, a), [P, PACK, PASS], F32) for g in range(G) for a in range(KP)}
+        w1_w = {(g, a): held("w1_w%d%d" % (g, a), [P, PASS], U32) for g in range(G) for a in range(KP)}
+        w1_s = {(g, a): held("w1_s%d%d" % (g, a), [P, PASS], U8) for g in range(G) for a in range(KP)}
+        h_w = [held("h_w%d" % g, [P, S], U32) for g in range(G)]
+        h_s = [held("h_s%d" % g, [P, S], U8) for g in range(G)]
+        square = {
+            (x, g, jt): held("square_%s%d%d" % (x, g, jt), [P, PACK, P], F32)
+            for x in "ab"
+            for g in range(G)
+            for jt in range(JT)
+        }
+
+        nc.vector.memset(tab_s[:].bitcast(I32), 0)
+        nc.vector.memset(one[:], 1.0)
+        nc.gpsimd.memset(w2_s[:].bitcast(I32), 0)
+        nc.gpsimd.memset(picked_s["b", 1][:].bitcast(I32), 0)
+        nc.gpsimd.memset(picked_s["a", 1][:].bitcast(I32), 0)
+        nc.gpsimd.memset(w3_s[:].bitcast(I32), 0)
+        make_identity(nc, ident[:])
+        nc.scalar.activation(zero[:], one[:], ACT.Ln)
+
+        def load_w2(g):
+            src = w2_words.rearrange("a p c i -> p a (c i)")[:, :, PACK * PASS * g : PACK * PASS * (g + 1)]
+            nc.sync.dma_start(w2_w[g][:].bitcast(I32), src.bitcast(I32))
+
+        def load_w1(g, a):
+            src = w1[PASS * a : PASS * (a + 1), PASS * g : PASS * (g + 1)]
+            nc.sync.dma_start(w1_raw[g, a][:], src.rearrange("(p i) c -> p i c", i=PACK))
+
+        def load_scales(plane, scales):
+            for q in range(4):
+                src = scales[:, 4 * q : 4 * q + 4, :].rearrange("a r c -> r a c")
+                nc.sync.dma_start(plane[32 * q : 32 * q + 4, :, :].bitcast(I32), src.bitcast(I32))
+
+        nc.sync.dma_start(list_b[:], offs2)
+        nc.sync.dma_start(tab_w[0][:].bitcast(I32), tab_words[0].bitcast(I32))
+        for q in range(4):
+            nc.sync.dma_start(
+                tab_s[32 * q : 32 * q + 4 * KP, :].bitcast(I32), tab_scales[:, 4 * q : 4 * q + 4, :].bitcast(I32)
+            )
+        nc.sync.dma_start(tab_w[1][:].bitcast(I32), tab_words[1].bitcast(I32))
+        nc.sync.dma_start(list_a[:], offs)
+        load_w2(0)
+        load_scales(w2_s, w2_scales)
+        load_w2(1)
+        load_w2(2)
+        load_w1(0, 0)
+        load_w1(0, 1)
+        nc.sync.dma_start(ground_t[:], ground.rearrange("(g p t) -> p g t", p=P, t=PACK))
+        nc.sync.dma_start(gain_t[:], gain.rearrange("(g p t) -> p g t", p=P, t=PACK))
+        for g in range(1, G):
+            for a in range(KP):
+                load_w1(g, a)
+        nc.sync.dma_start(w3_w[:].bitcast(I32), w3_words.rearrange("a p c -> p a c").bitcast(I32))
+        load_scales(w3_s, w3_scales)
+
+        def pick(x, offsets):
+            nc.vector.tensor_copy(picked_s[x, 0][:], tab_s[:].indirect(offsets[:]))
+            nc.scalar.dma_start(
+                picked_s[x, 1][0:SHIFT_ROWS, :].bitcast(I32), picked_s[x, 0][4 : 4 + SHIFT_ROWS, :].bitcast(I32)
+            )
+            for a in range(KP):
+                nc.vector.tensor_copy(picked_w[x, a][:], tab_w[a][:].indirect(offsets[:]))
+
+        def quantize_w1(g, a):
+            woven = ring.tile([P, PASS * PACK], BF16, name="w1_woven", align_bytes=64)
+            nc.vector.tensor_copy(
+                woven[:].rearrange("p (c e i) -> p c i e", e=RUN, i=PACK),
+                w1_raw[g, a][:].rearrange("p i (c e) -> p c i e", e=RUN),
+            )
+            nc.vector.quantize_mx(w1_w[g, a][:].bitcast(FP8X4), w1_s[g, a][:], woven[:])
+
+        def products(x, g, tiles):
+            banks = {jt: psum.tile([P, PASS], F32, name="sums") for jt in tiles}
+            for a in range(KP):
+                if x == "a":
+                    words, scales = w1_w[g, a][:], w1_s[g, a][:]
+                else:
+                    words, scales = w2_w[g][:, a, :], w2_s[:, a, PASS * g : PASS * (g + 1)]
+                for jt in tiles:
+                    cols = slice(P * jt, P * (jt + 1))
+                    nc.tensor.matmul_mx(
+                        banks[jt][:],
+                        lhsT=picked_w[x, a][:, cols].bitcast(FP4X4),
+                        lhsT_scale=picked_s[x, a][:, cols],
+                        rhs=words.bitcast(FP8X4),
+                        rhs_scale=scales,
+                        start=(a == 0),
+                        stop=(a == KP - 1),
+                    )
+            for jt in tiles:
+                nc.scalar.activation(
+                    square[x, g, jt][:], banks[jt][:].rearrange("p (m t) -> p t m", t=PACK), ACT.Square, bias=zero[:]
+                )
+
+        def make_h(g, half):
+            tiles = [2 * half, 2 * half + 1]
+            logs = ring.tile([P, PACK, 2 * P], F32, name="logs")
+            banks = [psum.tile([P, 2, 2 * P], F32, name="energy") for pair in range(2)]
+            steps = [(x, jt) for x in "ba" for jt in tiles]
+            for n, (x, jt) in enumerate(steps):
+                for t in range(PACK):
+                    nc.tensor.matmul(
+                        banks[t // 2][:, t % 2, P * (jt % 2) : P * (jt % 2 + 1)],
+                        lhsT=square[x, g, jt][:, t, :],
+                        rhs=ident[:],
+                        is_transpose=True,
+                        start=(n == 0 and t % 2 == 0),
+                        stop=(n == len(steps) - 1 and t % 2 == 1),
+                    )
+            for t in range(PACK):
+                nc.scalar.activation(logs[:, t, :], banks[t // 2][:, t % 2, :], ACT.Ln, bias=ground_t[:, g, t : t + 1])
+            woven = ring.tile([P, 2 * P * PACK], BF16, name="h_woven", align_bytes=64)
+            nc.vector.tensor_tensor(
+                woven[:].rearrange("p (c e t) -> p c t e", e=RUN, t=PACK),
+                logs[:].rearrange("p t (c e) -> p c t e", e=RUN),
+                gain_t[:, g, :].unsqueeze(1).unsqueeze(3).to_broadcast([P, 2 * P // RUN, PACK, RUN]),
+                MULT,
+            )
+            cols = slice(2 * P * half, 2 * P * (half + 1))
+            nc.vector.quantize_mx(h_w[g][:, cols].bitcast(FP8X4), h_s[g][:, cols], woven[:])
+
+        def finish(jt):
+            bank = psum.tile([P, NT, P], F32, name="sums")
+            cols = slice(P * jt, P * (jt + 1))
+            for g in range(G):
+                for n in range(NT):
+                    nc.tensor.matmul_mx(
+                        bank[:, n, :],
+                        lhsT=w3_w[:, g, 2 * P * n : 2 * P * (n + 1)].bitcast(FP4X4),
+                        lhsT_scale=w3_s[:, g, P * n : P * (n + 1)],
+                        rhs=h_w[g][:, cols].bitcast(FP8X4),
+                        rhs_scale=h_s[g][:, cols],
+                        start=(g == 0 and n == 0),
+                        stop=(g == G - 1 and n == NT - 1),
+                    )
+            result = keep.tile([P, NT, P], F32, name="result%d" % jt)
+            nc.scalar.copy(result[:], bank[:])
+            nc.sync.dma_start(out[:, cols].rearrange("(n p) j -> p n j", p=P), result[:])
+
+        pick("b", list_b)
+        pick("a", list_a)
+        for g in range(G):
+            products("b", g, range(JT))
+        for a in range(KP):
+            quantize_w1(0, a)
+        for g in range(G):
+            if g == 0:
+                products("a", g, range(JT))
+            for half in range(2):
+                if g > 0:
+                    products("a", g, [2 * half, 2 * half + 1])
+                if g + 1 < G:
+                    quantize_w1(g + 1, half)
+                make_h(g, half)
+        for jt in range(JT):
+            finish(jt)

@@ -25,7 +25,7 @@ G = H // PASS
 JT = S // P
 NT = N // P
 RUN = 4
-SHIFT_ROWS = 112
+PAIR = 2
 
 
 def tile_list_scour_priority_kernel(
@@ -43,7 +43,7 @@ def tile_list_scour_priority_kernel(
         list_a = keep.tile([P, S // 16], U16, name="list_a")
         list_b = keep.tile([P, S // 16], U16, name="list_b")
         tab_w = [held("tab_w%d" % a, [P, T], U16) for a in range(KP)]
-        tab_s = held("tab_s", [P, T], U8)
+        tab_s = held("tab_s", [P, KP, T], U8)
         w2_w = [held("w2_w%d" % g, [P, KP, PASS], U32) for g in range(G)]
         w2_s = held("w2_s", [P, KP, H], U8)
         w3_w = held("w3_w", [P, G, 2 * N], U8)
@@ -55,7 +55,15 @@ def tile_list_scour_priority_kernel(
         zero = held("zero", [P, 1], F32)
         picked_w = {(x, a): held("picked_w%s%d" % (x, a), [P, S], U16) for x in "ab" for a in range(KP)}
         picked_s = {(x, a): held("picked_s%s%d" % (x, a), [P, S], U8) for x in "ab" for a in range(KP)}
-        w1_raw = {(g, a): held("w1_raw%d%d" % (g, a), [P, PACK, PASS], F32) for g in range(G) for a in range(KP)}
+        parts = {(g, a): 1 for g in range(G) for a in range(KP)}
+        parts[0, KP - 1] = 2
+        parts[G - 1, KP - 1] = 2
+        w1_raw = {
+            (g, a, c): held("w1_raw%d%d%d" % (g, a, c), [P, PACK, PASS // parts[g, a]], F32)
+            for g in range(G)
+            for a in range(KP)
+            for c in range(parts[g, a])
+        }
         w1_w = {(g, a): held("w1_w%d%d" % (g, a), [P, PASS], U32) for g in range(G) for a in range(KP)}
         w1_s = {(g, a): held("w1_s%d%d" % (g, a), [P, PASS], U8) for g in range(G) for a in range(KP)}
         h_w = [held("h_w%d" % g, [P, S], U32) for g in range(G)]
@@ -67,11 +75,10 @@ def tile_list_scour_priority_kernel(
             for jt in range(JT)
         }
 
-        nc.vector.memset(tab_s[:].bitcast(I32), 0)
-        nc.vector.memset(one[:], 1.0)
-        nc.gpsimd.memset(w2_s[:].bitcast(I32), 0)
-        nc.gpsimd.memset(picked_s["b", 1][:].bitcast(I32), 0)
-        nc.gpsimd.memset(picked_s["a", 1][:].bitcast(I32), 0)
+        nc.gpsimd.memset(tab_s[:, 0, :].bitcast(I32), 0)
+        nc.vector.memset(tab_s[:, 1, :].bitcast(I32), 0)
+        nc.gpsimd.memset(one[:], 1.0)
+        nc.vector.memset(w2_s[:].bitcast(I32), 0)
         nc.gpsimd.memset(w3_s[:].bitcast(I32), 0)
         make_identity(nc, ident[:])
         nc.scalar.activation(zero[:], one[:], ACT.Ln)
@@ -81,54 +88,53 @@ def tile_list_scour_priority_kernel(
             nc.sync.dma_start(w2_w[g][:].bitcast(I32), src.bitcast(I32))
 
         def load_w1(g, a):
-            src = w1[PASS * a : PASS * (a + 1), PASS * g : PASS * (g + 1)]
-            nc.sync.dma_start(w1_raw[g, a][:], src.rearrange("(p i) c -> p i c", i=PACK))
+            width = PASS // parts[g, a]
+            for c in range(parts[g, a]):
+                first = PASS * g + width * c
+                src = w1[PASS * a : PASS * (a + 1), first : first + width]
+                nc.sync.dma_start(w1_raw[g, a, c][:], src.rearrange("(p i) c -> p i c", i=PACK))
 
-        def load_scales(plane, scales):
+        def load_scales(queue, plane, scales):
             for q in range(4):
                 src = scales[:, 4 * q : 4 * q + 4, :].rearrange("a r c -> r a c")
-                nc.sync.dma_start(plane[32 * q : 32 * q + 4, :, :].bitcast(I32), src.bitcast(I32))
+                queue.dma_start(plane[32 * q : 32 * q + 4, :, :].bitcast(I32), src.bitcast(I32))
 
         nc.sync.dma_start(list_b[:], offs2)
         nc.sync.dma_start(tab_w[0][:].bitcast(I32), tab_words[0].bitcast(I32))
-        for q in range(4):
-            nc.sync.dma_start(
-                tab_s[32 * q : 32 * q + 4 * KP, :].bitcast(I32), tab_scales[:, 4 * q : 4 * q + 4, :].bitcast(I32)
-            )
+        load_scales(nc.sync, tab_s, tab_scales)
         nc.sync.dma_start(tab_w[1][:].bitcast(I32), tab_words[1].bitcast(I32))
-        nc.sync.dma_start(list_a[:], offs)
         load_w2(0)
-        load_scales(w2_s, w2_scales)
+        load_scales(nc.sync, w2_s, w2_scales)
+        nc.sync.dma_start(list_a[:], offs)
         load_w2(1)
         load_w2(2)
-        load_w1(0, 0)
-        load_w1(0, 1)
-        nc.sync.dma_start(ground_t[:], ground.rearrange("(g p t) -> p g t", p=P, t=PACK))
-        nc.sync.dma_start(gain_t[:], gain.rearrange("(g p t) -> p g t", p=P, t=PACK))
-        for g in range(1, G):
+        for g in range(G):
             for a in range(KP):
                 load_w1(g, a)
+            if g == 0:
+                nc.sync.dma_start(ground_t[:], ground.rearrange("(g p t) -> p g t", p=P, t=PACK))
+                nc.sync.dma_start(gain_t[:], gain.rearrange("(g p t) -> p g t", p=P, t=PACK))
         nc.sync.dma_start(w3_w[:].bitcast(I32), w3_words.rearrange("a p c -> p a c").bitcast(I32))
-        load_scales(w3_s, w3_scales)
+        load_scales(nc.sync, w3_s, w3_scales)
 
         def pick(x, offsets):
-            nc.vector.tensor_copy(picked_s[x, 0][:], tab_s[:].indirect(offsets[:]))
-            nc.scalar.dma_start(
-                picked_s[x, 1][0:SHIFT_ROWS, :].bitcast(I32), picked_s[x, 0][4 : 4 + SHIFT_ROWS, :].bitcast(I32)
-            )
             for a in range(KP):
                 nc.vector.tensor_copy(picked_w[x, a][:], tab_w[a][:].indirect(offsets[:]))
+                nc.vector.tensor_copy(picked_s[x, a][:], tab_s[:, a, :].indirect(offsets[:]))
 
         def quantize_w1(g, a):
-            woven = ring.tile([P, PASS * PACK], BF16, name="w1_woven", align_bytes=64)
-            nc.vector.tensor_copy(
-                woven[:].rearrange("p (c e i) -> p c i e", e=RUN, i=PACK),
-                w1_raw[g, a][:].rearrange("p i (c e) -> p c i e", e=RUN),
-            )
-            nc.vector.quantize_mx(w1_w[g, a][:].bitcast(FP8X4), w1_s[g, a][:], woven[:])
+            width = PASS // parts[g, a]
+            for c in range(parts[g, a]):
+                woven = ring.tile([P, width * PACK], BF16, name="w1_woven", align_bytes=64)
+                nc.vector.tensor_copy(
+                    woven[:].rearrange("p (c e i) -> p c i e", e=RUN, i=PACK),
+                    w1_raw[g, a, c][:].rearrange("p i (c e) -> p c i e", e=RUN),
+                )
+                cols = slice(width * c, width * (c + 1))
+                nc.vector.quantize_mx(w1_w[g, a][:, cols].bitcast(FP8X4), w1_s[g, a][:, cols], woven[:])
 
-        def products(x, g, tiles):
-            banks = {jt: psum.tile([P, PASS], F32, name="sums") for jt in tiles}
+        def products(x, g, tiles, tag):
+            banks = {jt: psum.tile([P, PASS], F32, name=tag) for jt in tiles}
             for a in range(KP):
                 if x == "a":
                     words, scales = w1_w[g, a][:], w1_s[g, a][:]
@@ -147,34 +153,40 @@ def tile_list_scour_priority_kernel(
                     )
             for jt in tiles:
                 nc.scalar.activation(
-                    square[x, g, jt][:], banks[jt][:].rearrange("p (m t) -> p t m", t=PACK), ACT.Square, bias=zero[:]
+                    square[x, g, jt][:].rearrange("p t (c e) -> p c t e", e=RUN),
+                    banks[jt][:].rearrange("p (c e t) -> p c t e", e=RUN, t=PACK),
+                    ACT.Square,
+                    bias=zero[:],
                 )
 
-        def make_h(g, half):
-            tiles = [2 * half, 2 * half + 1]
-            logs = ring.tile([P, PACK, 2 * P], F32, name="logs")
-            banks = [psum.tile([P, 2, 2 * P], F32, name="energy") for pair in range(2)]
-            steps = [(x, jt) for x in "ba" for jt in tiles]
+        def make_h(g, tiles, steps):
+            width = P * len(tiles)
+            per_bank = PASS // width
+            logs = ring.tile([P, PACK, width], F32, name="logs")
+            banks = [psum.tile([P, per_bank, width], F32, name="energy") for n in range(PACK // per_bank)]
             for n, (x, jt) in enumerate(steps):
+                first = P * (jt - tiles[0])
                 for t in range(PACK):
                     nc.tensor.matmul(
-                        banks[t // 2][:, t % 2, P * (jt % 2) : P * (jt % 2 + 1)],
+                        banks[t // per_bank][:, t % per_bank, first : first + P],
                         lhsT=square[x, g, jt][:, t, :],
                         rhs=ident[:],
                         is_transpose=True,
-                        start=(n == 0 and t % 2 == 0),
-                        stop=(n == len(steps) - 1 and t % 2 == 1),
+                        start=(n == 0 and t % per_bank == 0),
+                        stop=(n == len(steps) - 1 and t % per_bank == per_bank - 1),
                     )
             for t in range(PACK):
-                nc.scalar.activation(logs[:, t, :], banks[t // 2][:, t % 2, :], ACT.Ln, bias=ground_t[:, g, t : t + 1])
-            woven = ring.tile([P, 2 * P * PACK], BF16, name="h_woven", align_bytes=64)
+                nc.scalar.activation(
+                    logs[:, t, :], banks[t // per_bank][:, t % per_bank, :], ACT.Ln, bias=ground_t[:, g, t : t + 1]
+                )
+            woven = ring.tile([P, width * PACK], BF16, name="h_woven", align_bytes=64)
             nc.vector.tensor_tensor(
-                woven[:].rearrange("p (c e t) -> p c t e", e=RUN, t=PACK),
-                logs[:].rearrange("p t (c e) -> p c t e", e=RUN),
-                gain_t[:, g, :].unsqueeze(1).unsqueeze(3).to_broadcast([P, 2 * P // RUN, PACK, RUN]),
+                woven[:].rearrange("p (c e t) -> p c t e", e=PAIR, t=PACK),
+                logs[:].rearrange("p t (c e) -> p c t e", e=PAIR),
+                gain_t[:, g, :].unsqueeze(1).unsqueeze(3).to_broadcast([P, width // PAIR, PACK, PAIR]),
                 MULT,
             )
-            cols = slice(2 * P * half, 2 * P * (half + 1))
+            cols = slice(P * tiles[0], P * tiles[0] + width)
             nc.vector.quantize_mx(h_w[g][:, cols].bitcast(FP8X4), h_s[g][:, cols], woven[:])
 
         def finish(jt):
@@ -198,17 +210,19 @@ def tile_list_scour_priority_kernel(
         pick("b", list_b)
         pick("a", list_a)
         for g in range(G):
-            products("b", g, range(JT))
+            products("b", g, range(JT), "energy" if g == 1 else "sums")
+        units = [(g, [2 * half, 2 * half + 1]) for g in range(G) for half in range(2)]
         for a in range(KP):
             quantize_w1(0, a)
-        for g in range(G):
-            if g == 0:
-                products("a", g, range(JT))
-            for half in range(2):
-                if g > 0:
-                    products("a", g, [2 * half, 2 * half + 1])
-                if g + 1 < G:
-                    quantize_w1(g + 1, half)
-                make_h(g, half)
+        products("a", *units[0], "sums")
+        for u, (g, tiles) in enumerate(units):
+            if g + 1 < G:
+                quantize_w1(g + 1, u % 2)
+            if u + 1 < len(units):
+                products("a", *units[u + 1], "sums")
+                make_h(g, tiles, [("b", jt) for jt in tiles] + [("a", jt) for jt in reversed(tiles)])
+            else:
+                for jt in tiles:
+                    make_h(g, [jt], [("b", jt), ("a", jt)])
         for jt in range(JT):
             finish(jt)

@@ -34,7 +34,7 @@ def tile_list_scour_priority_kernel(
     nc = tc.nc
     with ExitStack() as ctx:
         keep = ctx.enter_context(tc.tile_pool(name="keep", bufs=1))
-        ring = ctx.enter_context(tc.tile_pool(name="ring", bufs=3))
+        ring = ctx.enter_context(tc.tile_pool(name="ring", bufs=4))
         psum = ctx.enter_context(tc.psum_pool(name="psum", bufs=4))
 
         def held(name, shape, dtype):
@@ -56,7 +56,6 @@ def tile_list_scour_priority_kernel(
         picked_w = {(x, a): held("picked_w%s%d" % (x, a), [P, S], U16) for x in "ab" for a in range(KP)}
         picked_s = {(x, a): held("picked_s%s%d" % (x, a), [P, S], U8) for x in "ab" for a in range(KP)}
         parts = {(g, a): 1 for g in range(G) for a in range(KP)}
-        parts[0, KP - 1] = 2
         parts[G - 1, KP - 1] = 2
         w1_raw = {
             (g, a, c): held("w1_raw%d%d%d" % (g, a, c), [P, PACK, PASS // parts[g, a]], F32)
@@ -102,6 +101,8 @@ def tile_list_scour_priority_kernel(
         nc.sync.dma_start(list_b[:], offs2)
         nc.sync.dma_start(tab_w[0][:].bitcast(I32), tab_words[0].bitcast(I32))
         load_scales(nc.sync, tab_s, tab_scales)
+        nc.sync.dma_start(ground_t[:], ground.rearrange("(g p t) -> p g t", p=P, t=PACK))
+        nc.sync.dma_start(gain_t[:], gain.rearrange("(g p t) -> p g t", p=P, t=PACK))
         nc.sync.dma_start(tab_w[1][:].bitcast(I32), tab_words[1].bitcast(I32))
         load_w2(0)
         load_scales(nc.sync, w2_s, w2_scales)
@@ -111,9 +112,6 @@ def tile_list_scour_priority_kernel(
         for g in range(G):
             for a in range(KP):
                 load_w1(g, a)
-            if g == 0:
-                nc.sync.dma_start(ground_t[:], ground.rearrange("(g p t) -> p g t", p=P, t=PACK))
-                nc.sync.dma_start(gain_t[:], gain.rearrange("(g p t) -> p g t", p=P, t=PACK))
         nc.sync.dma_start(w3_w[:].bitcast(I32), w3_words.rearrange("a p c -> p a c").bitcast(I32))
         load_scales(nc.sync, w3_s, w3_scales)
 
@@ -123,15 +121,22 @@ def tile_list_scour_priority_kernel(
                 nc.vector.tensor_copy(picked_s[x, a][:], tab_s[:, a, :].indirect(offsets[:]))
 
         def quantize_w1(g, a):
-            width = PASS // parts[g, a]
-            for c in range(parts[g, a]):
-                woven = ring.tile([P, width * PACK], BF16, name="w1_woven", align_bytes=64)
+            half = PASS // 2
+            wovens = []
+            for c in range(2):
+                woven = ring.tile([P, half * PACK], BF16, name="w1_woven", align_bytes=64)
+                if parts[g, a] == 2:
+                    raw = w1_raw[g, a, c][:]
+                else:
+                    raw = w1_raw[g, a, 0][:, :, half * c : half * (c + 1)]
                 nc.vector.tensor_copy(
                     woven[:].rearrange("p (c e i) -> p c i e", e=RUN, i=PACK),
-                    w1_raw[g, a, c][:].rearrange("p i (c e) -> p c i e", e=RUN),
+                    raw.rearrange("p i (c e) -> p c i e", e=RUN),
                 )
-                cols = slice(width * c, width * (c + 1))
-                nc.vector.quantize_mx(w1_w[g, a][:, cols].bitcast(FP8X4), w1_s[g, a][:, cols], woven[:])
+                wovens.append(woven)
+            for c in range(2):
+                cols = slice(half * c, half * (c + 1))
+                nc.vector.quantize_mx(w1_w[g, a][:, cols].bitcast(FP8X4), w1_s[g, a][:, cols], wovens[c][:])
 
         def products(x, g, tiles, tag):
             banks = {jt: psum.tile([P, PASS], F32, name=tag) for jt in tiles}
@@ -179,15 +184,19 @@ def tile_list_scour_priority_kernel(
                 nc.scalar.activation(
                     logs[:, t, :], banks[t // per_bank][:, t % per_bank, :], ACT.Ln, bias=ground_t[:, g, t : t + 1]
                 )
-            woven = ring.tile([P, width * PACK], BF16, name="h_woven", align_bytes=64)
-            nc.vector.tensor_tensor(
-                woven[:].rearrange("p (c e t) -> p c t e", e=PAIR, t=PACK),
-                logs[:].rearrange("p t (c e) -> p c t e", e=PAIR),
-                gain_t[:, g, :].unsqueeze(1).unsqueeze(3).to_broadcast([P, width // PAIR, PACK, PAIR]),
-                MULT,
-            )
-            cols = slice(P * tiles[0], P * tiles[0] + width)
-            nc.vector.quantize_mx(h_w[g][:, cols].bitcast(FP8X4), h_s[g][:, cols], woven[:])
+            wovens = {}
+            for jt in tiles:
+                first = P * (jt - tiles[0])
+                wovens[jt] = ring.tile([P, P * PACK], BF16, name="h_woven", align_bytes=64)
+                nc.vector.tensor_tensor(
+                    wovens[jt][:].rearrange("p (c e t) -> p c t e", e=PAIR, t=PACK),
+                    logs[:, :, first : first + P].rearrange("p t (c e) -> p c t e", e=PAIR),
+                    gain_t[:, g, :].unsqueeze(1).unsqueeze(3).to_broadcast([P, P // PAIR, PACK, PAIR]),
+                    MULT,
+                )
+            for jt in tiles:
+                cols = slice(P * jt, P * (jt + 1))
+                nc.vector.quantize_mx(h_w[g][:, cols].bitcast(FP8X4), h_s[g][:, cols], wovens[jt][:])
 
         def finish(jt):
             bank = psum.tile([P, NT, P], F32, name="sums")
@@ -211,18 +220,14 @@ def tile_list_scour_priority_kernel(
         pick("a", list_a)
         for g in range(G):
             products("b", g, range(JT), "energy" if g == 1 else "sums")
-        units = [(g, [2 * half, 2 * half + 1]) for g in range(G) for half in range(2)]
-        for a in range(KP):
-            quantize_w1(0, a)
-        products("a", *units[0], "sums")
-        for u, (g, tiles) in enumerate(units):
-            if g + 1 < G:
-                quantize_w1(g + 1, u % 2)
-            if u + 1 < len(units):
-                products("a", *units[u + 1], "sums")
+        for g in range(G):
+            for a in range(KP):
+                quantize_w1(g, a)
+        for g in range(G):
+            products("a", g, range(JT), "sums")
+            size = 1 if g == G - 1 else 2
+            for first in range(0, JT, size):
+                tiles = list(range(first, first + size))
                 make_h(g, tiles, [("b", jt) for jt in tiles] + [("a", jt) for jt in reversed(tiles)])
-            else:
-                for jt in tiles:
-                    make_h(g, [jt], [("b", jt), ("a", jt)])
         for jt in range(JT):
             finish(jt)

@@ -78,7 +78,7 @@ def tile_list_scour_priority_kernel(
         nc.vector.memset(tab_s[:, 1, :].bitcast(I32), 0)
         nc.gpsimd.memset(one[:], 1.0)
         nc.vector.memset(w2_s[:].bitcast(I32), 0)
-        nc.gpsimd.memset(w3_s[:].bitcast(I32), 0)
+        nc.vector.memset(w3_s[:].bitcast(I32), 0)
         make_identity(nc, ident[:])
         nc.scalar.activation(zero[:], one[:], ACT.Ln)
 
@@ -94,9 +94,9 @@ def tile_list_scour_priority_kernel(
                 nc.sync.dma_start(w1_raw[g, a, c][:], src.rearrange("(p i) c -> p i c", i=PACK))
 
         def load_scales(queue, plane, scales):
-            for q in range(4):
-                src = scales[:, 4 * q : 4 * q + 4, :].rearrange("a r c -> r a c")
-                queue.dma_start(plane[32 * q : 32 * q + 4, :, :].bitcast(I32), src.bitcast(I32))
+            for r in range(4):
+                src = scales[:, r:16:4, :].rearrange("a q c -> q a c")
+                queue.dma_start(plane[r:P:32, :, :].bitcast(I32), src.bitcast(I32))
 
         nc.sync.dma_start(list_b[:], offs2)
         nc.sync.dma_start(tab_w[0][:].bitcast(I32), tab_words[0].bitcast(I32))
@@ -105,7 +105,7 @@ def tile_list_scour_priority_kernel(
         nc.sync.dma_start(gain_t[:], gain.rearrange("(g p t) -> p g t", p=P, t=PACK))
         nc.sync.dma_start(tab_w[1][:].bitcast(I32), tab_words[1].bitcast(I32))
         load_w2(0)
-        load_scales(nc.sync, w2_s, w2_scales)
+        load_scales(nc.gpsimd, w2_s, w2_scales)
         nc.sync.dma_start(list_a[:], offs)
         load_w2(1)
         load_w2(2)

@@ -50,6 +50,7 @@ def tile_list_scour_priority_kernel(
         w3_s = held("w3_s", [P, G, N], U8)
         ground_t = held("ground_t", [P, G, PACK], F32)
         gain_t = held("gain_t", [P, G, PACK], F32)
+        gain_pairs = held("gain_pairs", [P, G, PACK, PAIR], F32)
         ident = held("ident", [P, P], F32)
         one = held("one", [P, 1], F32)
         zero = held("zero", [P, 1], F32)
@@ -115,6 +116,8 @@ def tile_list_scour_priority_kernel(
         nc.sync.dma_start(w3_w[:].bitcast(I32), w3_words.rearrange("a p c -> p a c").bitcast(I32))
         load_scales(nc.sync, w3_s, w3_scales)
 
+        nc.scalar.copy(gain_pairs[:], gain_t[:].unsqueeze(3).to_broadcast([P, G, PACK, PAIR]))
+
         def pick(x, offsets):
             for a in range(KP):
                 nc.vector.tensor_copy(picked_w[x, a][:], tab_w[a][:].indirect(offsets[:]))
@@ -130,8 +133,8 @@ def tile_list_scour_priority_kernel(
                 else:
                     raw = w1_raw[g, a, 0][:, :, half * c : half * (c + 1)]
                 nc.vector.tensor_copy(
-                    woven[:].rearrange("p (c e i) -> p c i e", e=RUN, i=PACK),
-                    raw.rearrange("p i (c e) -> p c i e", e=RUN),
+                    woven[:].rearrange("p (c e i) -> p c i e", e=PAIR, i=PACK),
+                    raw.rearrange("p i (c e) -> p c i e", e=PAIR),
                 )
                 wovens.append(woven)
             for c in range(2):
@@ -191,7 +194,7 @@ def tile_list_scour_priority_kernel(
                 nc.vector.tensor_tensor(
                     wovens[jt][:].rearrange("p (c e t) -> p c t e", e=PAIR, t=PACK),
                     logs[:, :, first : first + P].rearrange("p t (c e) -> p c t e", e=PAIR),
-                    gain_t[:, g, :].unsqueeze(1).unsqueeze(3).to_broadcast([P, P // PAIR, PACK, PAIR]),
+                    gain_pairs[:, g, :, :].unsqueeze(1).to_broadcast([P, P // PAIR, PACK, PAIR]),
                     MULT,
                 )
             for jt in tiles:

@@ -35,7 +35,7 @@ def tile_list_scour_priority_kernel(
     with ExitStack() as ctx:
         keep = ctx.enter_context(tc.tile_pool(name="keep", bufs=1))
         ring = ctx.enter_context(tc.tile_pool(name="ring", bufs=4))
-        psum = ctx.enter_context(tc.psum_pool(name="psum", bufs=4))
+        psum = ctx.enter_context(tc.psum_pool(name="psum", bufs=1))
 
         def held(name, shape, dtype):
             return keep.tile(shape, dtype, name=name, align_bytes=64)
@@ -79,7 +79,7 @@ def tile_list_scour_priority_kernel(
         nc.vector.memset(tab_s[:, 1, :].bitcast(I32), 0)
         nc.gpsimd.memset(one[:], 1.0)
         nc.vector.memset(w2_s[:].bitcast(I32), 0)
-        nc.vector.memset(w3_s[:].bitcast(I32), 0)
+        nc.gpsimd.memset(w3_s[:].bitcast(I32), 0)
         make_identity(nc, ident[:])
         nc.scalar.activation(zero[:], one[:], ACT.Ln)
 
@@ -102,15 +102,17 @@ def tile_list_scour_priority_kernel(
         nc.sync.dma_start(list_b[:], offs2)
         nc.sync.dma_start(tab_w[0][:].bitcast(I32), tab_words[0].bitcast(I32))
         load_scales(nc.sync, tab_s, tab_scales)
-        nc.sync.dma_start(ground_t[:], ground.rearrange("(g p t) -> p g t", p=P, t=PACK))
-        nc.sync.dma_start(gain_t[:], gain.rearrange("(g p t) -> p g t", p=P, t=PACK))
         nc.sync.dma_start(tab_w[1][:].bitcast(I32), tab_words[1].bitcast(I32))
         load_w2(0)
-        load_scales(nc.gpsimd, w2_s, w2_scales)
-        nc.sync.dma_start(list_a[:], offs)
+        load_scales(nc.sync, w2_s, w2_scales)
         load_w2(1)
+        nc.sync.dma_start(list_a[:], offs)
         load_w2(2)
-        for g in range(G):
+        load_w1(0, 0)
+        load_w1(0, 1)
+        nc.sync.dma_start(ground_t[:], ground.rearrange("(g p t) -> p g t", p=P, t=PACK))
+        nc.sync.dma_start(gain_t[:], gain.rearrange("(g p t) -> p g t", p=P, t=PACK))
+        for g in range(1, G):
             for a in range(KP):
                 load_w1(g, a)
         nc.sync.dma_start(w3_w[:].bitcast(I32), w3_words.rearrange("a p c -> p a c").bitcast(I32))
@@ -141,68 +143,60 @@ def tile_list_scour_priority_kernel(
                 cols = slice(half * c, half * (c + 1))
                 nc.vector.quantize_mx(w1_w[g, a][:, cols].bitcast(FP8X4), w1_s[g, a][:, cols], wovens[c][:])
 
-        def products(x, g, tiles, tag):
-            banks = {jt: psum.tile([P, PASS], F32, name=tag) for jt in tiles}
+        def product(x, g, jt):
+            bank = psum.tile([P, PASS], F32, name="sums%d" % jt)
+            cols = slice(P * jt, P * (jt + 1))
             for a in range(KP):
                 if x == "a":
                     words, scales = w1_w[g, a][:], w1_s[g, a][:]
                 else:
                     words, scales = w2_w[g][:, a, :], w2_s[:, a, PASS * g : PASS * (g + 1)]
-                for jt in tiles:
-                    cols = slice(P * jt, P * (jt + 1))
-                    nc.tensor.matmul_mx(
-                        banks[jt][:],
-                        lhsT=picked_w[x, a][:, cols].bitcast(FP4X4),
-                        lhsT_scale=picked_s[x, a][:, cols],
-                        rhs=words.bitcast(FP8X4),
-                        rhs_scale=scales,
-                        start=(a == 0),
-                        stop=(a == KP - 1),
-                    )
-            for jt in tiles:
-                nc.scalar.activation(
-                    square[x, g, jt][:].rearrange("p t (c e) -> p c t e", e=RUN),
-                    banks[jt][:].rearrange("p (c e t) -> p c t e", e=RUN, t=PACK),
-                    ACT.Square,
-                    bias=zero[:],
+                nc.tensor.matmul_mx(
+                    bank[:],
+                    lhsT=picked_w[x, a][:, cols].bitcast(FP4X4),
+                    lhsT_scale=picked_s[x, a][:, cols],
+                    rhs=words.bitcast(FP8X4),
+                    rhs_scale=scales,
+                    start=(a == 0),
+                    stop=(a == KP - 1),
                 )
+            nc.scalar.activation(
+                square[x, g, jt][:].rearrange("p t (c e) -> p c t e", e=RUN),
+                bank[:].rearrange("p (c e t) -> p c t e", e=RUN, t=PACK),
+                ACT.Square,
+                bias=zero[:],
+            )
 
-        def make_h(g, tiles, steps):
-            width = P * len(tiles)
-            per_bank = PASS // width
-            logs = ring.tile([P, PACK, width], F32, name="logs")
-            banks = [psum.tile([P, per_bank, width], F32, name="energy") for n in range(PACK // per_bank)]
-            for n, (x, jt) in enumerate(steps):
-                first = P * (jt - tiles[0])
+        def make_h(g, jt):
+            logs = ring.tile([P, PACK, P], F32, name="logs")
+            bank = psum.tile([P, PACK, P], F32, name="energy%d" % jt)
+            for n, x in enumerate("ba"):
                 for t in range(PACK):
                     nc.tensor.matmul(
-                        banks[t // per_bank][:, t % per_bank, first : first + P],
+                        bank[:, t, :],
                         lhsT=square[x, g, jt][:, t, :],
                         rhs=ident[:],
                         is_transpose=True,
-                        start=(n == 0 and t % per_bank == 0),
-                        stop=(n == len(steps) - 1 and t % per_bank == per_bank - 1),
+                        start=(n == 0 and t == 0),
+                        stop=(n == 1 and t == PACK - 1),
                     )
             for t in range(PACK):
-                nc.scalar.activation(
-                    logs[:, t, :], banks[t // per_bank][:, t % per_bank, :], ACT.Ln, bias=ground_t[:, g, t : t + 1]
-                )
-            wovens = {}
-            for jt in tiles:
-                first = P * (jt - tiles[0])
-                wovens[jt] = ring.tile([P, P * PACK], BF16, name="h_woven", align_bytes=64)
-                nc.vector.tensor_tensor(
-                    wovens[jt][:].rearrange("p (c e t) -> p c t e", e=PAIR, t=PACK),
-                    logs[:, :, first : first + P].rearrange("p t (c e) -> p c t e", e=PAIR),
-                    gain_pairs[:, g, :, :].unsqueeze(1).to_broadcast([P, P // PAIR, PACK, PAIR]),
-                    MULT,
-                )
-            for jt in tiles:
-                cols = slice(P * jt, P * (jt + 1))
-                nc.vector.quantize_mx(h_w[g][:, cols].bitcast(FP8X4), h_s[g][:, cols], wovens[jt][:])
+                nc.scalar.activation(logs[:, t, :], bank[:, t, :], ACT.Ln, bias=ground_t[:, g, t : t + 1])
+            woven = ring.tile([P, P * PACK], BF16, name="h_woven", align_bytes=64)
+            nc.vector.tensor_tensor(
+                woven[:].rearrange("p (c e t) -> p c t e", e=PAIR, t=PACK),
+                logs[:].rearrange("p t (c e) -> p c t e", e=PAIR),
+                gain_pairs[:, g, :, :].unsqueeze(1).to_broadcast([P, P // PAIR, PACK, PAIR]),
+                MULT,
+            )
+            return woven
+
+        def quantize_h(g, jt, woven):
+            cols = slice(P * jt, P * (jt + 1))
+            nc.vector.quantize_mx(h_w[g][:, cols].bitcast(FP8X4), h_s[g][:, cols], woven[:])
 
         def finish(jt):
-            bank = psum.tile([P, NT, P], F32, name="sums")
+            bank = psum.tile([P, NT, P], F32, name="sums%d" % jt)
             cols = slice(P * jt, P * (jt + 1))
             for g in range(G):
                 for n in range(NT):
@@ -222,15 +216,21 @@ def tile_list_scour_priority_kernel(
         pick("b", list_b)
         pick("a", list_a)
         for g in range(G):
-            products("b", g, range(JT), "energy" if g == 1 else "sums")
+            for jt in range(JT):
+                product("b", g, jt)
         for g in range(G):
             for a in range(KP):
                 quantize_w1(g, a)
-        for g in range(G):
-            products("a", g, range(JT), "sums")
-            size = 1 if g == G - 1 else 2
-            for first in range(0, JT, size):
-                tiles = list(range(first, first + size))
-                make_h(g, tiles, [("b", jt) for jt in tiles] + [("a", jt) for jt in reversed(tiles)])
+        units = [(g, jt) for g in range(G) for jt in range(JT)]
+        product("a", *units[0])
+        waiting = None
+        for n, (g, jt) in enumerate(units):
+            if n + 1 < len(units):
+                product("a", *units[n + 1])
+            woven = make_h(g, jt)
+            if waiting is not None:
+                quantize_h(*waiting)
+            waiting = (g, jt, woven)
+        quantize_h(*waiting)
         for jt in range(JT):
             finish(jt)

@@ -16,6 +16,7 @@ FP8X4 = mybir.dt.float8_e4m3fn_x4
 FP4X4 = mybir.dt.float4_e2m1fn_x4
 ACT = mybir.ActivationFunctionType
 MULT = mybir.AluOpType.mult
+ADD = mybir.AluOpType.add
 
 P = 128
 PACK = 4
@@ -105,11 +106,11 @@ def tile_list_scour_priority_kernel(
         nc.sync.dma_start(tab_w[1][:].bitcast(I32), tab_words[1].bitcast(I32))
         load_w2(0)
         load_scales(nc.sync, w2_s, w2_scales)
-        load_w2(1)
         nc.sync.dma_start(list_a[:], offs)
-        load_w2(2)
         load_w1(0, 0)
+        load_w2(1)
         load_w1(0, 1)
+        load_w2(2)
         nc.sync.dma_start(ground_t[:], ground.rearrange("(g p t) -> p g t", p=P, t=PACK))
         nc.sync.dma_start(gain_t[:], gain.rearrange("(g p t) -> p g t", p=P, t=PACK))
         for g in range(1, G):
@@ -134,10 +135,15 @@ def tile_list_scour_priority_kernel(
                     raw = w1_raw[g, a, c][:]
                 else:
                     raw = w1_raw[g, a, 0][:, :, half * c : half * (c + 1)]
-                nc.vector.tensor_copy(
-                    woven[:].rearrange("p (c e i) -> p c i e", e=PAIR, i=PACK),
-                    raw.rearrange("p i (c e) -> p c i e", e=PAIR),
-                )
+                if g == 0 and (a, c) != (1, 1):
+                    nc.gpsimd.tensor_scalar(
+                        woven[:].rearrange("p (c i) -> p c i", i=PACK), raw.rearrange("p i c -> p c i"), 1.0, 0.0, MULT, ADD
+                    )
+                else:
+                    nc.vector.tensor_copy(
+                        woven[:].rearrange("p (c e i) -> p c i e", e=PAIR, i=PACK),
+                        raw.rearrange("p i (c e) -> p c i e", e=PAIR),
+                    )
                 wovens.append(woven)
             for c in range(2):
                 cols = slice(half * c, half * (c + 1))
@@ -167,29 +173,54 @@ def tile_list_scour_priority_kernel(
                 bias=zero[:],
             )
 
+        def turn(bank, x, g, jt, t, start, stop):
+            nc.tensor.matmul(
+                bank, lhsT=square[x, g, jt][:, t, :], rhs=ident[:], is_transpose=True, start=start, stop=stop
+            )
+
+        def weave_h(g, logs):
+            woven = ring.tile([P, P * PACK], BF16, name="h_woven", align_bytes=64)
+            nc.vector.tensor_tensor(
+                woven[:].rearrange("p (c e t) -> p c t e", e=PAIR, t=PACK),
+                logs.rearrange("p t (c e) -> p c t e", e=PAIR),
+                gain_pairs[:, g, :, :].unsqueeze(1).to_broadcast([P, P // PAIR, PACK, PAIR]),
+                MULT,
+            )
+            return woven
+
+        def wide_group(g):
+            banks = [psum.tile([P, JT, P], F32, name="energy%d" % t) for t in range(PACK)]
+            product("a", g, 0)
+            for jt in range(1, JT):
+                product("a", g, jt)
+                if jt < JT - 1:
+                    for t in (2 * jt - 2, 2 * jt - 1):
+                        for n in range(JT):
+                            turn(banks[t][:, n, :], "b", g, n, t, n == 0, False)
+            for jt in range(JT):
+                for t in range(PACK):
+                    turn(banks[t][:, jt, :], "a", g, jt, t, False, jt == JT - 1)
+            logs = keep.tile([P, PACK, S], F32, name="wide_logs%d" % g)
+            for t in range(PACK):
+                nc.scalar.activation(
+                    logs[:, t, :], banks[t][:].rearrange("p n j -> p (n j)"), ACT.Ln, bias=ground_t[:, g, t : t + 1]
+                )
+            wovens = []
+            for jt in range(JT):
+                wovens.append(weave_h(g, logs[:, :, P * jt : P * (jt + 1)]))
+                if jt > 0:
+                    quantize_h(g, jt - 1, wovens[jt - 1])
+            quantize_h(g, JT - 1, wovens[JT - 1])
+
         def make_h(g, jt):
             logs = ring.tile([P, PACK, P], F32, name="logs")
             bank = psum.tile([P, PACK, P], F32, name="energy%d" % jt)
             for n, x in enumerate("ba"):
                 for t in range(PACK):
-                    nc.tensor.matmul(
-                        bank[:, t, :],
-                        lhsT=square[x, g, jt][:, t, :],
-                        rhs=ident[:],
-                        is_transpose=True,
-                        start=(n == 0 and t == 0),
-                        stop=(n == 1 and t == PACK - 1),
-                    )
+                    turn(bank[:, t, :], x, g, jt, t, n == 0 and t == 0, n == 1 and t == PACK - 1)
             for t in range(PACK):
                 nc.scalar.activation(logs[:, t, :], bank[:, t, :], ACT.Ln, bias=ground_t[:, g, t : t + 1])
-            woven = ring.tile([P, P * PACK], BF16, name="h_woven", align_bytes=64)
-            nc.vector.tensor_tensor(
-                woven[:].rearrange("p (c e t) -> p c t e", e=PAIR, t=PACK),
-                logs[:].rearrange("p t (c e) -> p c t e", e=PAIR),
-                gain_pairs[:, g, :, :].unsqueeze(1).to_broadcast([P, P // PAIR, PACK, PAIR]),
-                MULT,
-            )
-            return woven
+            return weave_h(g, logs[:])
 
         def quantize_h(g, jt, woven):
             cols = slice(P * jt, P * (jt + 1))
@@ -221,7 +252,9 @@ def tile_list_scour_priority_kernel(
         for g in range(G):
             for a in range(KP):
                 quantize_w1(g, a)
-        units = [(g, jt) for g in range(G) for jt in range(JT)]
+        for g in range(G - 1):
+            wide_group(g)
+        units = [(G - 1, jt) for jt in range(JT)]
         product("a", *units[0])
         waiting = None
         for n, (g, jt) in enumerate(units):

@@ -51,7 +51,6 @@ def tile_list_scour_priority_kernel(
         w3_s = held("w3_s", [P, G, N], U8)
         ground_t = held("ground_t", [P, G, PACK], F32)
         gain_t = held("gain_t", [P, G, PACK], F32)
-        gain_pairs = held("gain_pairs", [P, G, PACK, PAIR], F32)
         ident = held("ident", [P, P], F32)
         one = held("one", [P, 1], F32)
         zero = held("zero", [P, 1], F32)
@@ -119,12 +118,14 @@ def tile_list_scour_priority_kernel(
         nc.sync.dma_start(w3_w[:].bitcast(I32), w3_words.rearrange("a p c -> p a c").bitcast(I32))
         load_scales(nc.sync, w3_s, w3_scales)
 
-        nc.scalar.copy(gain_pairs[:], gain_t[:].unsqueeze(3).to_broadcast([P, G, PACK, PAIR]))
-
-        def pick(x, offsets):
-            for a in range(KP):
-                nc.vector.tensor_copy(picked_w[x, a][:], tab_w[a][:].indirect(offsets[:]))
-                nc.vector.tensor_copy(picked_s[x, a][:], tab_s[:, a, :].indirect(offsets[:]))
+        def pick(x, offsets, cuts):
+            width = S // cuts
+            for c in range(cuts):
+                cols = slice(width * c, width * (c + 1))
+                entries = offsets[:, width * c // 16 : width * (c + 1) // 16]
+                for a in range(KP):
+                    nc.vector.tensor_copy(picked_w[x, a][:, cols], tab_w[a][:].indirect(entries))
+                    nc.vector.tensor_copy(picked_s[x, a][:, cols], tab_s[:, a, :].indirect(entries))
 
         def quantize_w1(g, a):
             half = PASS // 2
@@ -178,12 +179,12 @@ def tile_list_scour_priority_kernel(
                 bank, lhsT=square[x, g, jt][:, t, :], rhs=ident[:], is_transpose=True, start=start, stop=stop
             )
 
-        def weave_h(g, logs):
-            woven = ring.tile([P, P * PACK], BF16, name="h_woven", align_bytes=64)
+        def weave_h(g, logs, width):
+            woven = ring.tile([P, width * PACK], BF16, name="h_woven", align_bytes=64)
             nc.vector.tensor_tensor(
-                woven[:].rearrange("p (c e t) -> p c t e", e=PAIR, t=PACK),
-                logs.rearrange("p t (c e) -> p c t e", e=PAIR),
-                gain_pairs[:, g, :, :].unsqueeze(1).to_broadcast([P, P // PAIR, PACK, PAIR]),
+                woven[:].rearrange("p (c e t) -> p c t e", e=RUN, t=PACK),
+                logs.rearrange("p t (c e) -> p c t e", e=RUN),
+                gain_t[:, g, :].unsqueeze(1).unsqueeze(3).to_broadcast([P, width // RUN, PACK, RUN]),
                 MULT,
             )
             return woven
@@ -205,12 +206,10 @@ def tile_list_scour_priority_kernel(
                 nc.scalar.activation(
                     logs[:, t, :], banks[t][:].rearrange("p n j -> p (n j)"), ACT.Ln, bias=ground_t[:, g, t : t + 1]
                 )
-            wovens = []
-            for jt in range(JT):
-                wovens.append(weave_h(g, logs[:, :, P * jt : P * (jt + 1)]))
-                if jt > 0:
-                    quantize_h(g, jt - 1, wovens[jt - 1])
-            quantize_h(g, JT - 1, wovens[JT - 1])
+            halves = [slice(0, S // 2), slice(S // 2, S)]
+            wovens = [weave_h(g, logs[:, :, cols], S // 2) for cols in halves]
+            for cols, woven in zip(halves, wovens):
+                quantize_h(g, cols, woven)
 
         def make_h(g, jt):
             logs = ring.tile([P, PACK, P], F32, name="logs")
@@ -220,10 +219,9 @@ def tile_list_scour_priority_kernel(
                     turn(bank[:, t, :], x, g, jt, t, n == 0 and t == 0, n == 1 and t == PACK - 1)
             for t in range(PACK):
                 nc.scalar.activation(logs[:, t, :], bank[:, t, :], ACT.Ln, bias=ground_t[:, g, t : t + 1])
-            return weave_h(g, logs[:])
+            return weave_h(g, logs[:], P)
 
-        def quantize_h(g, jt, woven):
-            cols = slice(P * jt, P * (jt + 1))
+        def quantize_h(g, cols, woven):
             nc.vector.quantize_mx(h_w[g][:, cols].bitcast(FP8X4), h_s[g][:, cols], woven[:])
 
         def finish(jt):
@@ -244,8 +242,8 @@ def tile_list_scour_priority_kernel(
             nc.scalar.copy(result[:], bank[:])
             nc.sync.dma_start(out[:, cols].rearrange("(n p) j -> p n j", p=P), result[:])
 
-        pick("b", list_b)
-        pick("a", list_a)
+        pick("b", list_b, 2)
+        pick("a", list_a, 1)
         for g in range(G):
             for jt in range(JT):
                 product("b", g, jt)
@@ -263,7 +261,7 @@ def tile_list_scour_priority_kernel(
             woven = make_h(g, jt)
             if waiting is not None:
                 quantize_h(*waiting)
-            waiting = (g, jt, woven)
+            waiting = (g, slice(P * jt, P * (jt + 1)), woven)
         quantize_h(*waiting)
         for jt in range(JT):
             finish(jt)

@@ -151,7 +151,7 @@ def tile_list_scour_priority_kernel(
                 nc.vector.quantize_mx(w1_w[g, a][:, cols].bitcast(FP8X4), w1_s[g, a][:, cols], wovens[c][:])
 
         def product(x, g, jt):
-            bank = psum.tile([P, PASS], F32, name="sums%d" % jt)
+            bank = psum.tile([P, PASS], F32, name="bank%d" % (jt + JT * (g % 2 if x == "a" else 0)))
             cols = slice(P * jt, P * (jt + 1))
             for a in range(KP):
                 if x == "a":
@@ -171,7 +171,7 @@ def tile_list_scour_priority_kernel(
                 square[x, g, jt][:].rearrange("p t (c e) -> p c t e", e=RUN),
                 bank[:].rearrange("p (c e t) -> p c t e", e=RUN, t=PACK),
                 ACT.Square,
-                bias=zero[:],
+                bias=zero[:] if (x, g, jt) == ("b", 0, 0) else 0.0,
             )
 
         def turn(bank, x, g, jt, t, start, stop):
@@ -190,14 +190,12 @@ def tile_list_scour_priority_kernel(
             return woven
 
         def wide_group(g):
-            banks = [psum.tile([P, JT, P], F32, name="energy%d" % t) for t in range(PACK)]
-            product("a", g, 0)
-            for jt in range(1, JT):
+            banks = [psum.tile([P, JT, P], F32, name="bank%d" % (t + JT * (1 - g % 2))) for t in range(PACK)]
+            for t in range(PACK):
+                for jt in range(JT):
+                    turn(banks[t][:, jt, :], "b", g, jt, t, jt == 0, False)
+            for jt in range(JT):
                 product("a", g, jt)
-                if jt < JT - 1:
-                    for t in (2 * jt - 2, 2 * jt - 1):
-                        for n in range(JT):
-                            turn(banks[t][:, n, :], "b", g, n, t, n == 0, False)
             for jt in range(JT):
                 for t in range(PACK):
                     turn(banks[t][:, jt, :], "a", g, jt, t, False, jt == JT - 1)
@@ -213,7 +211,7 @@ def tile_list_scour_priority_kernel(
 
         def make_h(g, jt):
             logs = ring.tile([P, PACK, P], F32, name="logs")
-            bank = psum.tile([P, PACK, P], F32, name="energy%d" % jt)
+            bank = psum.tile([P, PACK, P], F32, name="bank%d" % (jt + JT * (1 - g % 2)))
             for n, x in enumerate("ba"):
                 for t in range(PACK):
                     turn(bank[:, t, :], x, g, jt, t, n == 0 and t == 0, n == 1 and t == PACK - 1)
@@ -225,7 +223,7 @@ def tile_list_scour_priority_kernel(
             nc.vector.quantize_mx(h_w[g][:, cols].bitcast(FP8X4), h_s[g][:, cols], woven[:])
 
         def finish(jt):
-            bank = psum.tile([P, NT, P], F32, name="sums%d" % jt)
+            bank = psum.tile([P, NT, P], F32, name="bank%d" % jt)
             cols = slice(P * jt, P * (jt + 1))
             for g in range(G):
                 for n in range(NT):

@@ -110,11 +110,12 @@ def tile_list_scour_priority_kernel(
         load_w2(1)
         load_w1(0, 1)
         load_w2(2)
+        load_w1(1, 0)
         nc.sync.dma_start(ground_t[:], ground.rearrange("(g p t) -> p g t", p=P, t=PACK))
+        load_w1(1, 1)
         nc.sync.dma_start(gain_t[:], gain.rearrange("(g p t) -> p g t", p=P, t=PACK))
-        for g in range(1, G):
-            for a in range(KP):
-                load_w1(g, a)
+        for a in range(KP):
+            load_w1(2, a)
         nc.sync.dma_start(w3_w[:].bitcast(I32), w3_words.rearrange("a p c -> p a c").bitcast(I32))
         load_scales(nc.sync, w3_s, w3_scales)
 
@@ -151,7 +152,7 @@ def tile_list_scour_priority_kernel(
                 nc.vector.quantize_mx(w1_w[g, a][:, cols].bitcast(FP8X4), w1_s[g, a][:, cols], wovens[c][:])
 
         def product(x, g, jt):
-            bank = psum.tile([P, PASS], F32, name="bank%d" % (jt + JT * (g % 2 if x == "a" else 0)))
+            bank = psum.tile([P, PASS], F32, name="bank%d" % (jt + JT * (g % 2)))
             cols = slice(P * jt, P * (jt + 1))
             for a in range(KP):
                 if x == "a":

@@ -241,6 +241,28 @@ def tile_list_scour_priority_kernel(
             nc.scalar.copy(result[:], bank[:])
             nc.sync.dma_start(out[:, cols].rearrange("(n p) j -> p n j", p=P), result[:])
 
+        def finish_last():
+            cols = slice(S - P, S)
+            banks = [psum.tile([P, P], F32, name="bank%d" % (JT - 1 + n)) for n in range(NT)]
+            for g in range(G):
+                for n in range(NT):
+                    nc.tensor.matmul_mx(
+                        banks[n][:],
+                        lhsT=w3_w[:, g, 2 * P * n : 2 * P * (n + 1)].bitcast(FP4X4),
+                        lhsT_scale=w3_s[:, g, P * n : P * (n + 1)],
+                        rhs=h_w[g][:, cols].bitcast(FP8X4),
+                        rhs_scale=h_s[g][:, cols],
+                        start=(g == 0),
+                        stop=(g == G - 1),
+                    )
+            for n in range(NT):
+                result = keep.tile([P, P], F32, name="last%d" % n)
+                if n == 1:
+                    nc.vector.tensor_copy(result[:], banks[n][:])
+                else:
+                    nc.scalar.copy(result[:], banks[n][:])
+                nc.sync.dma_start(out[P * n : P * (n + 1), cols], result[:])
+
         pick("b", list_b, 2)
         pick("a", list_a, 1)
         for g in range(G):
@@ -262,5 +284,6 @@ def tile_list_scour_priority_kernel(
                 quantize_h(*waiting)
             waiting = (g, slice(P * jt, P * (jt + 1)), woven)
         quantize_h(*waiting)
-        for jt in range(JT):
+        for jt in range(JT - 1):
             finish(jt)
+        finish_last()

from contextlib import ExitStack

import concourse.mybir as mybir
from concourse.masks import make_identity

K, T, S, H, N = 1024, 2048, 512, 1536, 384
FLOPS = 2 * (2 * K * H * S + H * N * S)

F32 = mybir.dt.float32
BF16 = mybir.dt.bfloat16
I32 = mybir.dt.int32
U32 = mybir.dt.uint32
U16 = mybir.dt.uint16
U8 = mybir.dt.uint8
FP8X4 = mybir.dt.float8_e4m3fn_x4
FP4X4 = mybir.dt.float4_e2m1fn_x4
ACT = mybir.ActivationFunctionType
MULT = mybir.AluOpType.mult
ADD = mybir.AluOpType.add

P = 128
PACK = 4
PASS = P * PACK
KP = K // PASS
G = H // PASS
JT = S // P
NT = N // P
RUN = 4
PAIR = 2


def tile_list_scour_priority_kernel(
    tc, tab_words, tab_scales, offs, offs2, w1, w2_words, w2_scales, ground, gain, w3_words, w3_scales, out
):
    nc = tc.nc
    with ExitStack() as ctx:
        keep = ctx.enter_context(tc.tile_pool(name="keep", bufs=1))
        ring = ctx.enter_context(tc.tile_pool(name="ring", bufs=4))
        psum = ctx.enter_context(tc.psum_pool(name="psum", bufs=1))

        def held(name, shape, dtype):
            return keep.tile(shape, dtype, name=name, align_bytes=64)

        list_a = keep.tile([P, S // 16], U16, name="list_a")
        list_b = keep.tile([P, S // 16], U16, name="list_b")
        tab_w = [held("tab_w%d" % a, [P, T], U16) for a in range(KP)]
        tab_s = held("tab_s", [P, KP, T], U8)
        w2_w = [held("w2_w%d" % g, [P, KP, PASS], U32) for g in range(G)]
        w2_s = held("w2_s", [P, KP, H], U8)
        w3_w = held("w3_w", [P, G, 2 * N], U8)
        w3_s = held("w3_s", [P, G, N], U8)
        ground_t = held("ground_t", [P, G, PACK], F32)
        gain_t = held("gain_t", [P, G, PACK], F32)
        ident = held("ident", [P, P], F32)
        one = held("one", [P, 1], F32)
        zero = held("zero", [P, 1], F32)
        picked_w = {(x, a): held("picked_w%s%d" % (x, a), [P, S], U16) for x in "ab" for a in range(KP)}
        picked_s = {(x, a): held("picked_s%s%d" % (x, a), [P, S], U8) for x in "ab" for a in range(KP)}
        parts = {(g, a): 1 for g in range(G) for a in range(KP)}
        parts[G - 1, KP - 1] = 2
        w1_raw = {
            (g, a, c): held("w1_raw%d%d%d" % (g, a, c), [P, PACK, PASS // parts[g, a]], F32)
            for g in range(G)
            for a in range(KP)
            for c in range(parts[g, a])
        }
        w1_w = {(g, a): held("w1_w%d%d" % (g, a), [P, PASS], U32) for g in range(G) for a in range(KP)}
        w1_s = {(g, a): held("w1_s%d%d" % (g, a), [P, PASS], U8) for g in range(G) for a in range(KP)}
        h_w = [held("h_w%d" % g, [P, S], U32) for g in range(G)]
        h_s = [held("h_s%d" % g, [P, S], U8) for g in range(G)]
        square = {
            (x, g, jt): held("square_%s%d%d" % (x, g, jt), [P, PACK, P], F32)
            for x in "ab"
            for g in range(G)
            for jt in range(JT)
        }

        nc.gpsimd.memset(tab_s[:, 0, :].bitcast(I32), 0)
        nc.vector.memset(tab_s[:, 1, :].bitcast(I32), 0)
        nc.gpsimd.memset(one[:], 1.0)
        nc.vector.memset(w2_s[:].bitcast(I32), 0)
        nc.gpsimd.memset(w3_s[:].bitcast(I32), 0)
        make_identity(nc, ident[:])
        nc.scalar.activation(zero[:], one[:], ACT.Ln)

        def load_w2(g):
            src = w2_words.rearrange("a p c i -> p a (c i)")[:, :, PACK * PASS * g : PACK * PASS * (g + 1)]
            nc.sync.dma_start(w2_w[g][:].bitcast(I32), src.bitcast(I32))

        def load_w1(g, a):
            width = PASS // parts[g, a]
            for c in range(parts[g, a]):
                first = PASS * g + width * c
                src = w1[PASS * a : PASS * (a + 1), first : first + width]
                nc.sync.dma_start(w1_raw[g, a, c][:], src.rearrange("(p i) c -> p i c", i=PACK))

        def load_scales(queue, plane, scales):
            for r in range(4):
                src = scales[:, r:16:4, :].rearrange("a q c -> q a c")
                queue.dma_start(plane[r:P:32, :, :].bitcast(I32), src.bitcast(I32))

        nc.sync.dma_start(list_b[:], offs2)
        nc.sync.dma_start(tab_w[0][:].bitcast(I32), tab_words[0].bitcast(I32))
        load_scales(nc.sync, tab_s, tab_scales)
        nc.sync.dma_start(tab_w[1][:].bitcast(I32), tab_words[1].bitcast(I32))
        load_w2(0)
        load_scales(nc.sync, w2_s, w2_scales)
        nc.sync.dma_start(list_a[:], offs)
        load_w1(0, 0)
        load_w2(1)
        load_w1(0, 1)
        load_w2(2)
        load_w1(1, 0)
        nc.sync.dma_start(ground_t[:], ground.rearrange("(g p t) -> p g t", p=P, t=PACK))
        load_w1(1, 1)
        nc.sync.dma_start(gain_t[:], gain.rearrange("(g p t) -> p g t", p=P, t=PACK))
        for a in range(KP):
            load_w1(2, a)
        nc.sync.dma_start(w3_w[:].bitcast(I32), w3_words.rearrange("a p c -> p a c").bitcast(I32))
        load_scales(nc.sync, w3_s, w3_scales)

        def pick(x, offsets, cuts):
            width = S // cuts
            for c in range(cuts):
                cols = slice(width * c, width * (c + 1))
                entries = offsets[:, width * c // 16 : width * (c + 1) // 16]
                for a in range(KP):
                    nc.vector.tensor_copy(picked_w[x, a][:, cols], tab_w[a][:].indirect(entries))
                    nc.vector.tensor_copy(picked_s[x, a][:, cols], tab_s[:, a, :].indirect(entries))

        def quantize_w1(g, a):
            half = PASS // 2
            wovens = []
            for c in range(2):
                woven = ring.tile([P, half * PACK], BF16, name="w1_woven", align_bytes=64)
                if parts[g, a] == 2:
                    raw = w1_raw[g, a, c][:]
                else:
                    raw = w1_raw[g, a, 0][:, :, half * c : half * (c + 1)]
                if g == 0 and (a, c) != (1, 1):
                    nc.gpsimd.tensor_scalar(
                        woven[:].rearrange("p (c i) -> p c i", i=PACK), raw.rearrange("p i c -> p c i"), 1.0, 0.0, MULT, ADD
                    )
                else:
                    nc.vector.tensor_copy(
                        woven[:].rearrange("p (c e i) -> p c i e", e=PAIR, i=PACK),
                        raw.rearrange("p i (c e) -> p c i e", e=PAIR),
                    )
                wovens.append(woven)
            for c in range(2):
                cols = slice(half * c, half * (c + 1))
                nc.vector.quantize_mx(w1_w[g, a][:, cols].bitcast(FP8X4), w1_s[g, a][:, cols], wovens[c][:])

        def product(x, g, jt):
            bank = psum.tile([P, PASS], F32, name="bank%d" % (jt + JT * (g % 2)))
            cols = slice(P * jt, P * (jt + 1))
            for a in range(KP):
                if x == "a":
                    words, scales = w1_w[g, a][:], w1_s[g, a][:]
                else:
                    words, scales = w2_w[g][:, a, :], w2_s[:, a, PASS * g : PASS * (g + 1)]
                nc.tensor.matmul_mx(
                    bank[:],
                    lhsT=picked_w[x, a][:, cols].bitcast(FP4X4),
                    lhsT_scale=picked_s[x, a][:, cols],
                    rhs=words.bitcast(FP8X4),
                    rhs_scale=scales,
                    start=(a == 0),
                    stop=(a == KP - 1),
                )
            nc.scalar.activation(
                square[x, g, jt][:].rearrange("p t (c e) -> p c t e", e=RUN),
                bank[:].rearrange("p (c e t) -> p c t e", e=RUN, t=PACK),
                ACT.Square,
                bias=zero[:] if (x, g, jt) == ("b", 0, 0) else 0.0,
            )

        def turn(bank, x, g, jt, t, start, stop):
            nc.tensor.matmul(
                bank, lhsT=square[x, g, jt][:, t, :], rhs=ident[:], is_transpose=True, start=start, stop=stop
            )

        def weave_h(g, logs, width):
            woven = ring.tile([P, width * PACK], BF16, name="h_woven", align_bytes=64)
            nc.vector.tensor_tensor(
                woven[:].rearrange("p (c e t) -> p c t e", e=RUN, t=PACK),
                logs.rearrange("p t (c e) -> p c t e", e=RUN),
                gain_t[:, g, :].unsqueeze(1).unsqueeze(3).to_broadcast([P, width // RUN, PACK, RUN]),
                MULT,
            )
            return woven

        def wide_group(g):
            banks = [psum.tile([P, JT, P], F32, name="bank%d" % (t + JT * (1 - g % 2))) for t in range(PACK)]
            for t in range(PACK):
                for jt in range(JT):
                    turn(banks[t][:, jt, :], "b", g, jt, t, jt == 0, False)
            for jt in range(JT):
                product("a", g, jt)
            for jt in range(JT):
                for t in range(PACK):
                    turn(banks[t][:, jt, :], "a", g, jt, t, False, jt == JT - 1)
            logs = keep.tile([P, PACK, S], F32, name="wide_logs%d" % g)
            for t in range(PACK):
                nc.scalar.activation(
                    logs[:, t, :], banks[t][:].rearrange("p n j -> p (n j)"), ACT.Ln, bias=ground_t[:, g, t : t + 1]
                )
            halves = [slice(0, S // 2), slice(S // 2, S)]
            wovens = [weave_h(g, logs[:, :, cols], S // 2) for cols in halves]
            for cols, woven in zip(halves, wovens):
                quantize_h(g, cols, woven)

        def make_h(g, jt):
            logs = ring.tile([P, PACK, P], F32, name="logs")
            bank = psum.tile([P, PACK, P], F32, name="bank%d" % (jt + JT * (1 - g % 2)))
            for n, x in enumerate("ba"):
                for t in range(PACK):
                    turn(bank[:, t, :], x, g, jt, t, n == 0 and t == 0, n == 1 and t == PACK - 1)
            for t in range(PACK):
                nc.scalar.activation(logs[:, t, :], bank[:, t, :], ACT.Ln, bias=ground_t[:, g, t : t + 1])
            return weave_h(g, logs[:], P)

        def quantize_h(g, cols, woven):
            nc.vector.quantize_mx(h_w[g][:, cols].bitcast(FP8X4), h_s[g][:, cols], woven[:])

        def finish(jt):
            bank = psum.tile([P, NT, P], F32, name="bank%d" % jt)
            cols = slice(P * jt, P * (jt + 1))
            for g in range(G):
                for n in range(NT):
                    nc.tensor.matmul_mx(
                        bank[:, n, :],
                        lhsT=w3_w[:, g, 2 * P * n : 2 * P * (n + 1)].bitcast(FP4X4),
                        lhsT_scale=w3_s[:, g, P * n : P * (n + 1)],
                        rhs=h_w[g][:, cols].bitcast(FP8X4),
                        rhs_scale=h_s[g][:, cols],
                        start=(g == 0 and n == 0),
                        stop=(g == G - 1 and n == NT - 1),
                    )
            result = keep.tile([P, NT, P], F32, name="result%d" % jt)
            nc.scalar.copy(result[:], bank[:])
            nc.sync.dma_start(out[:, cols].rearrange("(n p) j -> p n j", p=P), result[:])

        def finish_last():
            cols = slice(S - P, S)
            banks = [psum.tile([P, P], F32, name="bank%d" % (JT - 1 + n)) for n in range(NT)]
            for g in range(G):
                for n in range(NT):
                    nc.tensor.matmul_mx(
                        banks[n][:],
                        lhsT=w3_w[:, g, 2 * P * n : 2 * P * (n + 1)].bitcast(FP4X4),
                        lhsT_scale=w3_s[:, g, P * n : P * (n + 1)],
                        rhs=h_w[g][:, cols].bitcast(FP8X4),
                        rhs_scale=h_s[g][:, cols],
                        start=(g == 0),
                        stop=(g == G - 1),
                    )
            for n in range(NT):
                result = keep.tile([P, P], F32, name="last%d" % n)
                if n == 1:
                    nc.vector.tensor_copy(result[:], banks[n][:])
                else:
                    nc.scalar.copy(result[:], banks[n][:])
                nc.sync.dma_start(out[P * n : P * (n + 1), cols], result[:])

        pick("b", list_b, 2)
        pick("a", list_a, 1)
        for g in range(G):
            for jt in range(JT):
                product("b", g, jt)
        for g in range(G):
            for a in range(KP):
                quantize_w1(g, a)
        for g in range(G - 1):
            wide_group(g)
        units = [(G - 1, jt) for jt in range(JT)]
        product("a", *units[0])
        waiting = None
        for n, (g, jt) in enumerate(units):
            if n + 1 < len(units):
                product("a", *units[n + 1])
            woven = make_h(g, jt)
            if waiting is not None:
                quantize_h(*waiting)
            waiting = (g, slice(P * jt, P * (jt + 1)), woven)
        quantize_h(*waiting)
        for jt in range(JT - 1):
            finish(jt)
        finish_last()
